import numpy as np
import ml_dtypes


def mxq(x, axis, fmt="e4m3"):
    dtype, down = {"e4m3": (ml_dtypes.float8_e4m3fn, 7), "e5m2": (ml_dtypes.float8_e5m2, 14)}[fmt]
    v = np.moveaxis(np.asarray(x, np.float32).astype(ml_dtypes.bfloat16).astype(np.float64), axis, -1)
    blocks = v.reshape(v.shape[:-1] + (-1, 32))
    amax = np.abs(blocks).max(-1, keepdims=True)
    byte = np.maximum(np.where(amax > 0, np.frexp(amax)[1] - 1 + 127, 0) - down, 1)
    scale = np.exp2(byte - 127.0)
    codes = (blocks / scale).astype(np.float32).astype(dtype).astype(np.float64)
    return np.moveaxis((codes * scale).reshape(v.shape), -1, axis)


WIDE = False


def mx_kscale(k):
    if not WIDE:
        return np.ones(k)
    levels = np.array([10, -10, 5, -5, 0])
    if k % 512:
        return np.exp2(np.random.permutation(np.resize(levels, k // 32))).repeat(32)
    a = np.empty((k // 512, 16))
    for p in range(k // 512):
        a[p, :8] = np.random.permutation(np.resize(levels, 8))
        for g in range(8):
            far = levels[np.abs(levels - a[p, g]) >= 10]
            a[p, g + 8] = far[np.random.randint(len(far))]
    return np.exp2(a.ravel()).repeat(32)


def f64(x):
    return np.asarray(x).astype(np.float64)


def striped(idx):
    return np.tile(idx.reshape(-1, 16).T, (8, 1)).astype(np.uint16)


def unstriped(offs):
    return offs[:16].T.reshape(-1).astype(np.int64)


E2M1 = np.array([0.0, 0.5, 1.0, 1.5, 2.0, 3.0, 4.0, 6.0, -0.0, -0.5, -1.0, -1.5, -2.0, -3.0, -4.0, -6.0])


def pack_weight(w, fmt):
    k, n = w.shape
    w = f64(np.asarray(w, np.float32).astype(ml_dtypes.bfloat16)).reshape(k // 32, 32, n)
    amax = np.abs(w).max(1)
    if fmt == "e4m3":
        byte = np.frexp(amax)[1] - 1 + 127 - 7
    else:
        mant, ex = np.frexp(amax / 6.0)
        byte = np.where(mant > 0.5, ex, ex - 1) + 127
    byte = np.clip(np.where(amax > 0, byte, 1), 1, 254)
    scaled = (w * np.exp2(127.0 - byte)[:, None, :]).reshape(k, n).astype(np.float32)
    by_word = np.ascontiguousarray(scaled.reshape(k // 512, 128, 4, n).transpose(0, 1, 3, 2))
    if fmt == "e4m3":
        words = by_word.astype(ml_dtypes.float8_e4m3fn).view(np.uint8)
    else:
        c = by_word.astype(ml_dtypes.float4_e2m1fn).view(np.uint8) & 0xF
        words = (c[..., 0::2] | (c[..., 1::2] << 4)).reshape(k // 512, 128, 2 * n)
    return np.ascontiguousarray(words), np.ascontiguousarray(byte.astype(np.uint8).reshape(k // 512, 16, n))


def unpack_weight(words, scales, fmt):
    g, _, n = scales.shape
    words = np.ascontiguousarray(words).reshape(g, 128, n, -1)
    if fmt == "e4m3":
        vals = words.view(ml_dtypes.float8_e4m3fn).astype(np.float64)
    else:
        nib = np.empty((g, 128, n, 4), np.uint8)
        nib[..., 0::2] = words & 0xF
        nib[..., 1::2] = words >> 4
        vals = E2M1[nib]
    vals = vals * np.repeat(np.exp2(scales.astype(np.float64) - 127.0), 8, axis=1)[..., None]
    return vals.transpose(0, 1, 3, 2).reshape(g * 512, n)


def gelu(v):
    return 0.5 * v * (1.0 + np.tanh(np.sqrt(2.0 / np.pi) * (v + 0.044715 * v**3)))


K, T, S, H, T2, P = 1536, 4096, 1024, 1024, 2048, 512

def setup_inputs():
    n = np.random.standard_normal
    s = mx_kscale(K)[:, None]
    u = mx_kscale(H)[:, None]
    d = {}
    d["tab_words"], d["tab_scales"] = pack_weight(n((K, T)) * s, "e4m3")
    d["offs"] = striped(np.random.permutation(T)[:S])
    d["w1"] = (3.0 * n((K, H)) / K**0.5 / s).astype(np.float32)
    d["gain"] = (np.exp(0.3 * n(H)) * u[:, 0]).astype(np.float32)
    d["page0"] = (n((H, T2)) * u).astype(np.float32)
    d["wgs"] = np.exp(0.3 * n((128, S))).astype(np.float32)
    d["offs2"] = striped(np.random.permutation(T2)[:S])
    d["offs3"] = striped(np.random.permutation(T2)[:P])
    d["sc"] = (np.exp(0.3 * n(H)) / u[:, 0]).astype(np.float32)
    d["tg"] = (-2.0 * np.exp(0.3 * n(H)) * u[:, 0]).astype(np.float32)
    d["w2_words"], d["w2_scales"] = pack_weight(n((H, H)) / H**0.5 / u, "e2m1")
    d["w3"] = (n((H, H)) / H**0.5 / u).astype(np.float32)
    d["offs4"] = striped(np.random.permutation(T2)[:P])
    d["gf"] = (np.exp(0.3 * n(H)) / u[:, 0]).astype(np.float32)
    return d

def reference(tab_words, tab_scales, offs, w1, gain, page0, wgs, offs2, offs3, sc, tg,
              w2_words, w2_scales, w3, offs4, gf):
    v = unpack_weight(tab_words, tab_scales, "e4m3")[:, unstriped(offs)]
    f = mxq(f64(w1), 0, "e4m3").T @ v
    h = f64(gain)[:, None] * np.log(1.0 + np.abs(f))
    page = f64(page0).copy()
    page[:, unstriped(offs2)] = np.tile(f64(wgs), (H // 128, 1)) * h
    x = page[:, unstriped(offs3)]
    t = f64(tg)[:, None] * np.tanh(f64(sc)[:, None] * x)
    w2 = unpack_weight(w2_words, w2_scales, "e2m1")
    diff = w2.T @ mxq(x, 0, "e4m3") + mxq(f64(w3), 0, "e4m3").T @ mxq(t, 0, "e4m3")
    forest = f64(gf)[:, None] * page[:, unstriped(offs4)]
    return np.abs(diff) + forest

@@ -1,0 +1,261 @@
+from contextlib import ExitStack
+
+import concourse.mybir as mybir
+from concourse.masks import make_identity
+
+K, T, S, H, T2, M = 1536, 4096, 1024, 1024, 2048, 512
+FLOPS = 2 * K * H * S + 2 * 2 * H * H * M
+
+F32 = mybir.dt.float32
+BF16 = mybir.dt.bfloat16
+I32 = mybir.dt.int32
+U32 = mybir.dt.uint32
+U16 = mybir.dt.uint16
+U8 = mybir.dt.uint8
+FP8X4 = mybir.dt.float8_e4m3fn_x4
+FP4X4 = mybir.dt.float4_e2m1fn_x4
+ACT = mybir.ActivationFunctionType
+ALU = mybir.AluOpType
+
+P = 128
+PACK = 4
+KP = P * PACK
+PASSES1 = K // KP
+PASSES2 = H // KP
+SLICES = H // P
+PAIRS = SLICES // 2
+BANK = 512
+KB = 1024
+ROW = M + M // 2
+
+
+def tile_list_cork_lot_board_kernel(tc, tab_words, tab_scales, offs, w1, gain, page0, wgs, offs2, offs3,
+                                             sc, tg, w2_words, w2_scales, w3, offs4, gf, out):
+    nc = tc.nc
+    with ExitStack() as ctx:
+        lists = ctx.enter_context(tc.tile_pool(name="lists", bufs=1))
+        keep = ctx.enter_context(tc.tile_pool(name="keep", bufs=1))
+        shared = ctx.enter_context(tc.tile_pool(name="shared", bufs=1))
+        psum = ctx.enter_context(tc.psum_pool(name="psum", bufs=1))
+
+        o1 = lists.tile([P, S // 16], U16, name="o1")
+        o2 = lists.tile([P, S // 16], U16, name="o2")
+        o3 = lists.tile([P, M // 16], U16, name="o3")
+        o4 = lists.tile([P, M // 16], U16, name="o4")
+
+        banks = [psum.tile([P, BANK], F32, name="bank%d" % n) for n in range(8)]
+
+        def held(name, width, dtype):
+            return keep.tile([P, width], dtype, name=name, align_bytes=64)
+
+        def placed(name, width, dtype, kib):
+            return shared.tile([P, width], dtype, name=name, align_bytes=64, offset=kib * KB)
+
+        wg = [held("wg%d" % c, S, F32) for c in range(SLICES)]
+        h = [held("h%d" % c, S, F32) for c in range(SLICES)]
+        vec_rows = held("vec_rows", P, F32)
+        ident = held("ident", P, F32)
+        cols = held("cols", 4 * SLICES, F32)
+        tab_sc = held("tab_sc", T, U8)
+        got_sc = held("got_sc", S, U8)
+        got = [held("got%d" % a, S, U32) for a in range(PASSES1)]
+        w1_codes = [held("w1c%d" % c, PASSES1 * P, U32) for c in range(SLICES)]
+        w1_sc = [held("w1s%d" % c, PASSES1 * P, U8) for c in range(SLICES)]
+        w2_codes = held("w2c", PASSES2 * 2 * H, U8)
+        w2_sc = held("w2s", PASSES2 * H, U8)
+        w3_codes = [held("w3c%d" % b, H, U32) for b in range(PASSES2)]
+        w3_sc = [held("w3s%d" % b, H, U8) for b in range(PASSES2)]
+        x_codes = [held("xc%d" % b, M, U32) for b in range(PASSES2)]
+        x_sc = [held("xs%d" % b, M, U8) for b in range(PASSES2)]
+        t_codes = [held("tc%d" % b, M, U32) for b in range(PASSES2)]
+        t_sc = [held("ts%d" % b, M, U8) for b in range(PASSES2)]
+        work0 = held("work0", 3 * KB, F32)
+        work1 = held("work1", 4 * KB, F32)
+        stage = held("stage", 3 * KB, F32)
+        w3_bf1 = held("w3bf1", PACK * H, BF16)
+
+        gain_col, sc_col, tg_col, gf_col = [
+            [cols[:, SLICES * v + c: SLICES * v + c + 1] for c in range(SLICES)] for v in range(4)]
+
+        def load_w1(pair, raw):
+            for a in range(PASSES1):
+                nc.sync.dma_start(
+                    out=raw[:, KB * a: KB * (a + 1)].rearrange("p (i n) -> p i n", i=PACK),
+                    in_=w1[KP * a: KP * (a + 1), 2 * P * pair: 2 * P * (pair + 1)].rearrange("(p i) n -> p i n", i=PACK))
+
+        def load_page(c, kib):
+            page = placed("page%d" % c, T2, F32, kib)
+            nc.sync.dma_start(out=page[:], in_=page0[P * c: P * (c + 1), :])
+            return page
+
+        def load_w3(b, raw):
+            nc.sync.dma_start(out=raw[:], in_=w3[KP * b: KP * (b + 1), :].rearrange("(p i) n -> p (i n)", i=PACK))
+
+        def w1_bf(c):
+            width = PASSES1 * KP
+            return stage[:].bitcast(BF16)[:, width * (c % 4): width * (c % 4 + 1)]
+
+        def round_w1(pair, raw):
+            for s in range(2):
+                rows = raw[:, 0: 3 * KB].rearrange("p (a i s c j) -> p s a c i j", a=PASSES1, i=PACK, s=2, j=4)
+                nc.scalar.copy(out=w1_bf(2 * pair + s).rearrange("p (a c j i) -> p a c i j", a=PASSES1, j=4, i=PACK),
+                               in_=rows[:, s])
+            for s in range(2):
+                c = 2 * pair + s
+                nc.vector.quantize_mx(out=w1_codes[c][:].bitcast(FP8X4), scales=w1_sc[c][:], in_=w1_bf(c))
+
+        def interleave(dst, rows):
+            nc.scalar.copy(out=dst.rearrange("p (c j i) -> p c i j", j=4, i=PACK),
+                           in_=rows.rearrange("p i (c j) -> p c i j", j=4))
+
+        nc.vector.memset(vec_rows[:], 0.0)
+        nc.vector.memset(tab_sc[:].bitcast(I32), 0)
+        nc.vector.memset(w2_sc[:].bitcast(I32), 0)
+        nc.sync.dma_start(o1[:], offs)
+        nc.sync.dma_start(out=wg[SLICES - 1][:], in_=wgs)
+        for v, vec in enumerate((gain, sc, tg, gf)):
+            nc.scalar.dma_start(out=vec_rows[SLICES * v: SLICES * (v + 1), :], in_=vec.rearrange("(c p) -> c p", p=P))
+        make_identity(nc, ident[:])
+        for q in range(4):
+            nc.scalar.dma_start(out=tab_sc[32 * q: 32 * q + 4 * PASSES1, :].bitcast(I32),
+                                in_=tab_scales[:, 4 * q: 4 * q + 4, :].bitcast(I32))
+        for q in range(4):
+            nc.sync.dma_start(out=w2_sc[32 * q: 32 * q + 4, :].bitcast(I32).rearrange("r (b n) -> r b n", b=PASSES2),
+                                in_=w2_scales[:, 4 * q: 4 * q + 4, :].rearrange("b r n -> r b n").bitcast(I32))
+        load_w1(0, work0)
+        tab = [placed("tab%d" % a, T, U32, 16 * a) for a in range(PASSES1)]
+        for a in range(PASSES1):
+            nc.sync.dma_start(out=tab[a][:].bitcast(I32), in_=tab_words[a].rearrange("p t i -> p (t i)").bitcast(I32))
+        pages = {0: load_page(0, 48)}
+        nc.sync.dma_start(o2[:], offs2)
+        load_w1(1, work1)
+        pages[1] = load_page(1, 56)
+        nc.sync.dma_start(o3[:], offs3)
+        nc.sync.dma_start(o4[:], offs4)
+        nc.sync.dma_start(out=w2_codes[:].bitcast(I32).rearrange("p (b n) -> p b n", b=PASSES2),
+                          in_=w2_words.rearrange("b p n -> p b n").bitcast(I32))
+
+        nc.tensor.transpose(banks[7][:, 0:P], vec_rows[:], ident[:])
+        nc.scalar.copy(out=cols[:], in_=banks[7][:, 0: 4 * SLICES])
+        round_w1(0, work0)
+        for c in range(SLICES):
+            nc.scalar.activation(out=wg[c][:], in_=wg[SLICES - 1][:], func=ACT.Copy, scale=gain_col[c])
+
+        first_pieces = ((0, 256), (256, 512), (512, 1024))
+        nc.vector.tensor_copy(out=got_sc[:], in_=tab_sc[:].indirect(o1[:]))
+        for a in range(PASSES1 - 1):
+            nc.vector.tensor_copy(out=got[a][:], in_=tab[a][:].indirect(o1[:]))
+        for lo, hi in first_pieces:
+            nc.vector.tensor_copy(out=got[PASSES1 - 1][:, lo:hi],
+                                  in_=tab[PASSES1 - 1][:].indirect(o1[:, lo // 16: hi // 16]))
+
+        work2 = placed("work2", 4 * KB, F32, 0)
+        load_w1(2, work2)
+        pages[2] = load_page(2, 16)
+        work3 = placed("work3", 3 * KB, F32, 32)
+        load_w1(3, work3)
+        pages[3] = load_page(3, 24)
+        raws = {1: work1, 2: work2, 3: work3}
+
+        forest = {}
+        next_bank = 0
+        for c in range(SLICES):
+            if c in raws:
+                round_w1(c, raws[c])
+                mag = raws[c][:, 0:S]
+            elif c in (4, 5):
+                mag = work3[:, S * (c - 3): S * (c - 2)]
+            elif c == 6:
+                mag = w3_bf1[:].bitcast(F32)[:, 0:S]
+            elif c == SLICES - 1:
+                mag = stage[:, 0:S]
+            else:
+                mag = h[c][:]
+            pieces = first_pieces if c == 0 else ((0, BANK), (BANK, S))
+            for lo, hi in pieces:
+                acc = banks[next_bank % 8][:, 0: hi - lo]
+                next_bank = next_bank + 1
+                for a in range(PASSES1):
+                    nc.tensor.matmul_mx(out=acc, lhsT=w1_codes[c][:, P * a: P * (a + 1)].bitcast(FP8X4),
+                                        lhsT_scale=w1_sc[c][:, P * a: P * (a + 1)],
+                                        rhs=got[a][:, lo:hi].bitcast(FP8X4), rhs_scale=got_sc[4 * a: P, lo:hi],
+                                        start=(a == 0), stop=(a == PASSES1 - 1))
+                nc.scalar.activation(out=mag[:, lo:hi], in_=acc, func=ACT.Abs)
+                if c == 0:
+                    nc.scalar.activation(out=h[c][:, lo:hi], in_=mag[:, lo:hi], func=ACT.Ln, bias=1.0)
+                    nc.vector.tensor_tensor(pages[c][:].indirect(o2[:, lo // 16: hi // 16]), h[c][:, lo:hi],
+                                            wg[c][:, lo:hi], ALU.mult)
+            if c > 0:
+                nc.scalar.activation(out=h[c][:], in_=mag, func=ACT.Ln, bias=1.0)
+                nc.vector.tensor_tensor(pages[c][:].indirect(o2[:]), h[c][:], wg[c][:], ALU.mult)
+            nc.vector.tensor_copy(out=h[c][:, 0:M], in_=pages[c][:].indirect(o3[:]))
+            if c < 3:
+                forest[c] = wg[c][:, 0:M]
+                nc.vector.tensor_copy(out=forest[c], in_=pages[c][:].indirect(o4[:]))
+            if c == 0:
+                pages[4] = load_page(4, 48)
+            if c == 1:
+                load_w3(0, work1)
+                pages[5] = load_page(5, 56)
+            if c == 2:
+                load_w3(1, work2)
+                pages[6] = load_page(6, 16)
+            if c == 5:
+                pages[7] = load_page(7, 32)
+
+        dealt = (work0, stage)
+        w3_bf = (placed("w3bf0", PACK * H, BF16, 40), w3_bf1)
+        w3_raw = (work1, work2)
+
+        def tanh_and_deal(c):
+            th = stage[:, 0:M] if c <= 4 else work0[:, M: 2 * M]
+            nc.scalar.activation(out=th, in_=h[c][:, 0:M], func=ACT.Tanh, scale=sc_col[c])
+            nc.scalar.activation(out=h[c][:, M:ROW].bitcast(BF16), in_=th, func=ACT.Copy, scale=tg_col[c])
+            q = c % 4
+            nc.sync.dma_start(out=dealt[c // 4][32 * q: 32 * (q + 1), :].rearrange("p (i m) -> p i m", i=PACK),
+                              in_=h[c][:, 0:ROW])
+
+        def second_stage(b):
+            x_bf = work2[:, KB * b: KB * (b + 1)].bitcast(BF16)
+            t_bf = work1[:, KB * b: KB * (b + 1)].bitcast(BF16)
+            interleave(x_bf, dealt[b][:].rearrange("p (i m) -> p i m", i=PACK)[:, :, 0:M])
+            interleave(t_bf, dealt[b][:].bitcast(BF16).rearrange("p (i m) -> p i m", i=PACK)[:, :, 2 * M: 3 * M])
+            nc.vector.quantize_mx(out=x_codes[b][:].bitcast(FP8X4), scales=x_sc[b][:], in_=x_bf)
+            nc.vector.quantize_mx(out=t_codes[b][:].bitcast(FP8X4), scales=t_sc[b][:], in_=t_bf)
+            for n in range(SLICES):
+                nc.tensor.matmul_mx(out=banks[n][:],
+                                    lhsT=w2_codes[:, 2 * (H * b + P * n): 2 * (H * b + P * (n + 1))].bitcast(FP4X4),
+                                    lhsT_scale=w2_sc[:, H * b + P * n: H * b + P * (n + 1)],
+                                    rhs=x_codes[b][:].bitcast(FP8X4), rhs_scale=x_sc[b][:],
+                                    start=(b == 0), stop=False)
+            for n in range(SLICES):
+                nc.tensor.matmul_mx(out=banks[n][:], lhsT=w3_codes[b][:, P * n: P * (n + 1)].bitcast(FP8X4),
+                                    lhsT_scale=w3_sc[b][:, P * n: P * (n + 1)],
+                                    rhs=t_codes[b][:].bitcast(FP8X4), rhs_scale=t_sc[b][:],
+                                    start=False, stop=(b == PASSES2 - 1))
+
+        def pick_forest(c, dst):
+            forest[c] = dst
+            nc.vector.tensor_copy(out=dst, in_=pages[c][:].indirect(o4[:]))
+
+        for c in range(4):
+            tanh_and_deal(c)
+        for b in range(PASSES2):
+            interleave(w3_bf[b][:], w3_raw[b][:].rearrange("p (i n) -> p i n", i=PACK))
+            nc.vector.quantize_mx(out=w3_codes[b][:].bitcast(FP8X4), scales=w3_sc[b][:], in_=w3_bf[b][:])
+        tanh_and_deal(4)
+        second_stage(0)
+        for c in range(5, SLICES):
+            tanh_and_deal(c)
+        pick_forest(3, work2[:, 0:M])
+        pick_forest(4, work2[:, M: 2 * M])
+        pick_forest(5, work1[:, 0:M])
+        pick_forest(6, work1[:, M: 2 * M])
+        second_stage(1)
+        pick_forest(7, work1[:, 2 * M: 3 * M])
+
+        for n in range(SLICES):
+            nc.scalar.activation(out=wg[n][:, M:S], in_=banks[n][:], func=ACT.Abs)
+            nc.vector.scalar_tensor_tensor(out=h[n][:, 0:M], in0=forest[n], scalar=gf_col[n], in1=wg[n][:, M:S],
+                                           op0=ALU.mult, op1=ALU.add)
+            nc.sync.dma_start(out=out[P * n: P * (n + 1), :], in_=h[n][:, 0:M])

@@ -51,7 +51,7 @@ def tile_list_cork_lot_board_kernel(tc, tab_words, tab_scales, offs, w1, gain, p
         def placed(name, width, dtype, kib):
             return shared.tile([P, width], dtype, name=name, align_bytes=64, offset=kib * KB)
 
-        wg = [held("wg%d" % c, S, F32) for c in range(SLICES)]
+        wg = [held("wg%d" % c, S, F32) for c in range(SLICES - 1)] + [placed("wgs", S, F32, 72)]
         h = [held("h%d" % c, S, F32) for c in range(SLICES)]
         vec_rows = held("vec_rows", P, F32)
         ident = held("ident", P, F32)
@@ -64,15 +64,11 @@ def tile_list_cork_lot_board_kernel(tc, tab_words, tab_scales, offs, w1, gain, p
         w2_codes = held("w2c", PASSES2 * 2 * H, U8)
         w2_sc = held("w2s", PASSES2 * H, U8)
         w3_codes = [held("w3c%d" % b, H, U32) for b in range(PASSES2)]
-        w3_sc = [held("w3s%d" % b, H, U8) for b in range(PASSES2)]
         x_codes = [held("xc%d" % b, M, U32) for b in range(PASSES2)]
-        x_sc = [held("xs%d" % b, M, U8) for b in range(PASSES2)]
         t_codes = [held("tc%d" % b, M, U32) for b in range(PASSES2)]
-        t_sc = [held("ts%d" % b, M, U8) for b in range(PASSES2)]
         work0 = held("work0", 3 * KB, F32)
         work1 = held("work1", 4 * KB, F32)
         stage = held("stage", 3 * KB, F32)
-        w3_bf1 = held("w3bf1", PACK * H, BF16)
 
         gain_col, sc_col, tg_col, gf_col = [
             [cols[:, SLICES * v + c: SLICES * v + c + 1] for c in range(SLICES)] for v in range(4)]
@@ -87,6 +83,12 @@ def tile_list_cork_lot_board_kernel(tc, tab_words, tab_scales, offs, w1, gain, p
             page = placed("page%d" % c, T2, F32, kib)
             nc.sync.dma_start(out=page[:], in_=page0[P * c: P * (c + 1), :])
             return page
+
+        def load_table(a, words):
+            nc.sync.dma_start(out=words[:].bitcast(I32), in_=tab_words[a].rearrange("p t i -> p (t i)").bitcast(I32))
+
+        def load_vector(v, vec):
+            nc.sync.dma_start(out=vec_rows[SLICES * v: SLICES * (v + 1), :], in_=vec.rearrange("(c p) -> c p", p=P))
 
         def load_w3(b, raw):
             nc.sync.dma_start(out=raw[:], in_=w3[KP * b: KP * (b + 1), :].rearrange("(p i) n -> p (i n)", i=PACK))
@@ -108,35 +110,30 @@ def tile_list_cork_lot_board_kernel(tc, tab_words, tab_scales, offs, w1, gain, p
             nc.scalar.copy(out=dst.rearrange("p (c j i) -> p c i j", j=4, i=PACK),
                            in_=rows.rearrange("p i (c j) -> p c i j", j=4))
 
-        nc.vector.memset(vec_rows[:], 0.0)
         nc.vector.memset(tab_sc[:].bitcast(I32), 0)
+        nc.vector.memset(vec_rows[:], 0.0)
         nc.vector.memset(w2_sc[:].bitcast(I32), 0)
         nc.sync.dma_start(o1[:], offs)
-        nc.sync.dma_start(out=wg[SLICES - 1][:], in_=wgs)
-        for v, vec in enumerate((gain, sc, tg, gf)):
-            nc.scalar.dma_start(out=vec_rows[SLICES * v: SLICES * (v + 1), :], in_=vec.rearrange("(c p) -> c p", p=P))
-        make_identity(nc, ident[:])
-        for q in range(4):
-            nc.scalar.dma_start(out=tab_sc[32 * q: 32 * q + 4 * PASSES1, :].bitcast(I32),
-                                in_=tab_scales[:, 4 * q: 4 * q + 4, :].bitcast(I32))
-        for q in range(4):
-            nc.sync.dma_start(out=w2_sc[32 * q: 32 * q + 4, :].bitcast(I32).rearrange("r (b n) -> r b n", b=PASSES2),
-                                in_=w2_scales[:, 4 * q: 4 * q + 4, :].rearrange("b r n -> r b n").bitcast(I32))
-        load_w1(0, work0)
-        tab = [placed("tab%d" % a, T, U32, 16 * a) for a in range(PASSES1)]
-        for a in range(PASSES1):
-            nc.sync.dma_start(out=tab[a][:].bitcast(I32), in_=tab_words[a].rearrange("p t i -> p (t i)").bitcast(I32))
-        pages = {0: load_page(0, 48)}
         nc.sync.dma_start(o2[:], offs2)
-        load_w1(1, work1)
-        pages[1] = load_page(1, 56)
         nc.sync.dma_start(o3[:], offs3)
         nc.sync.dma_start(o4[:], offs4)
-        nc.sync.dma_start(out=w2_codes[:].bitcast(I32).rearrange("p (b n) -> p b n", b=PASSES2),
-                          in_=w2_words.rearrange("b p n -> p b n").bitcast(I32))
+        nc.sync.dma_start(out=wg[SLICES - 1][:], in_=wgs)
+        load_w1(0, work0)
+        tab = [placed("tab%d" % a, T, U32, 16 * a) for a in range(PASSES1)]
+        load_table(0, tab[0])
+        load_vector(0, gain)
+        for q in range(4):
+            nc.sync.dma_start(out=tab_sc[32 * q: 32 * q + 4 * PASSES1, :].bitcast(I32),
+                              in_=tab_scales[:, 4 * q: 4 * q + 4, :].bitcast(I32))
+        load_table(1, tab[1])
+        load_table(2, tab[2])
+        pages = {0: load_page(0, 48)}
+        load_w1(1, work1)
+        pages[1] = load_page(1, 56)
 
+        make_identity(nc, ident[:])
         nc.tensor.transpose(banks[7][:, 0:P], vec_rows[:], ident[:])
-        nc.scalar.copy(out=cols[:], in_=banks[7][:, 0: 4 * SLICES])
+        nc.scalar.copy(out=cols[:, 0:SLICES], in_=banks[7][:, 0:SLICES])
         round_w1(0, work0)
         for c in range(SLICES):
             nc.scalar.activation(out=wg[c][:], in_=wg[SLICES - 1][:], func=ACT.Copy, scale=gain_col[c])
@@ -155,6 +152,11 @@ def tile_list_cork_lot_board_kernel(tc, tab_words, tab_scales, offs, w1, gain, p
         work3 = placed("work3", 3 * KB, F32, 32)
         load_w1(3, work3)
         pages[3] = load_page(3, 24)
+        nc.sync.dma_start(out=w2_codes[:].bitcast(I32).rearrange("p (b n) -> p b n", b=PASSES2),
+                          in_=w2_words.rearrange("b p n -> p b n").bitcast(I32))
+        for q in range(4):
+            nc.sync.dma_start(out=w2_sc[32 * q: 32 * q + 4, :].bitcast(I32).rearrange("r (b n) -> r b n", b=PASSES2),
+                              in_=w2_scales[:, 4 * q: 4 * q + 4, :].rearrange("b r n -> r b n").bitcast(I32))
         raws = {1: work1, 2: work2, 3: work3}
 
         forest = {}
@@ -163,12 +165,8 @@ def tile_list_cork_lot_board_kernel(tc, tab_words, tab_scales, offs, w1, gain, p
             if c in raws:
                 round_w1(c, raws[c])
                 mag = raws[c][:, 0:S]
-            elif c in (4, 5):
-                mag = work3[:, S * (c - 3): S * (c - 2)]
-            elif c == 6:
-                mag = w3_bf1[:].bitcast(F32)[:, 0:S]
-            elif c == SLICES - 1:
-                mag = stage[:, 0:S]
+            elif c > 3:
+                mag = work3[:, S * (c % 3): S * (c % 3 + 1)]
             else:
                 mag = h[c][:]
             pieces = first_pieces if c == 0 else ((0, BANK), (BANK, S))
@@ -200,15 +198,20 @@ def tile_list_cork_lot_board_kernel(tc, tab_words, tab_scales, offs, w1, gain, p
             if c == 2:
                 load_w3(1, work2)
                 pages[6] = load_page(6, 16)
-            if c == 5:
-                pages[7] = load_page(7, 32)
+                pages[7] = load_page(7, 64)
 
+        for v, vec in enumerate((sc, tg, gf)):
+            load_vector(v + 1, vec)
+        nc.tensor.transpose(banks[7][:, 0:P], vec_rows[:], ident[:])
+        nc.scalar.copy(out=cols[:, SLICES: 4 * SLICES], in_=banks[7][:, SLICES: 4 * SLICES])
         dealt = (work0, stage)
-        w3_bf = (placed("w3bf0", PACK * H, BF16, 40), w3_bf1)
+        w3_sc = [placed("w3s%d" % b, H, U8, 72 + b) for b in range(PASSES2)]
+        x_sc = [placed("xs0", M, U8, 74), held("xs1", M, U8)]
+        t_sc = [placed("ts0", M, U8, 75), held("ts1", M, U8)]
         w3_raw = (work1, work2)
 
         def tanh_and_deal(c):
-            th = stage[:, 0:M] if c <= 4 else work0[:, M: 2 * M]
+            th = work3[:, S: S + M] if c < 4 else work0[:, M: 2 * M]
             nc.scalar.activation(out=th, in_=h[c][:, 0:M], func=ACT.Tanh, scale=sc_col[c])
             nc.scalar.activation(out=h[c][:, M:ROW].bitcast(BF16), in_=th, func=ACT.Copy, scale=tg_col[c])
             q = c % 4
@@ -240,12 +243,12 @@ def tile_list_cork_lot_board_kernel(tc, tab_words, tab_scales, offs, w1, gain, p
 
         for c in range(4):
             tanh_and_deal(c)
+        w3_bf = [placed("w3bf%d" % b, PACK * H, BF16, 32 + 8 * b) for b in range(PASSES2)]
         for b in range(PASSES2):
             interleave(w3_bf[b][:], w3_raw[b][:].rearrange("p (i n) -> p i n", i=PACK))
             nc.vector.quantize_mx(out=w3_codes[b][:].bitcast(FP8X4), scales=w3_sc[b][:], in_=w3_bf[b][:])
-        tanh_and_deal(4)
         second_stage(0)
-        for c in range(5, SLICES):
+        for c in range(4, SLICES):
             tanh_and_deal(c)
         pick_forest(3, work2[:, 0:M])
         pick_forest(4, work2[:, M: 2 * M])
@@ -255,7 +258,8 @@ def tile_list_cork_lot_board_kernel(tc, tab_words, tab_scales, offs, w1, gain, p
         pick_forest(7, work1[:, 2 * M: 3 * M])
 
         for n in range(SLICES):
-            nc.scalar.activation(out=wg[n][:, M:S], in_=banks[n][:], func=ACT.Abs)
-            nc.vector.scalar_tensor_tensor(out=h[n][:, 0:M], in0=forest[n], scalar=gf_col[n], in1=wg[n][:, M:S],
+            mag = wg[n][:, M:S] if n < SLICES - 1 else wg[n - 1][:, 0:M]
+            nc.scalar.activation(out=mag, in_=banks[n][:], func=ACT.Abs)
+            nc.vector.scalar_tensor_tensor(out=h[n][:, 0:M], in0=forest[n], scalar=gf_col[n], in1=mag,
                                            op0=ALU.mult, op1=ALU.add)
             nc.sync.dma_start(out=out[P * n: P * (n + 1), :], in_=h[n][:, 0:M])

from contextlib import ExitStack

import concourse.mybir as mybir
from concourse.masks import make_identity

K, T, S, H, T2, M = 1536, 4096, 1024, 1024, 2048, 512
FLOPS = 2 * K * H * S + 2 * 2 * H * H * M

F32 = mybir.dt.float32
BF16 = mybir.dt.bfloat16
I32 = mybir.dt.int32
U32 = mybir.dt.uint32
U16 = mybir.dt.uint16
U8 = mybir.dt.uint8
FP8X4 = mybir.dt.float8_e4m3fn_x4
FP4X4 = mybir.dt.float4_e2m1fn_x4
ACT = mybir.ActivationFunctionType
ALU = mybir.AluOpType

P = 128
PACK = 4
KP = P * PACK
PASSES1 = K // KP
PASSES2 = H // KP
SLICES = H // P
PAIRS = SLICES // 2
BANK = 512
KB = 1024
ROW = M + M // 2


def tile_list_cork_lot_board_kernel(tc, tab_words, tab_scales, offs, w1, gain, page0, wgs, offs2, offs3,
                                             sc, tg, w2_words, w2_scales, w3, offs4, gf, out):
    nc = tc.nc
    with ExitStack() as ctx:
        lists = ctx.enter_context(tc.tile_pool(name="lists", bufs=1))
        keep = ctx.enter_context(tc.tile_pool(name="keep", bufs=1))
        shared = ctx.enter_context(tc.tile_pool(name="shared", bufs=1))
        psum = ctx.enter_context(tc.psum_pool(name="psum", bufs=1))

        o1 = lists.tile([P, S // 16], U16, name="o1")
        o2 = lists.tile([P, S // 16], U16, name="o2")
        o3 = lists.tile([P, M // 16], U16, name="o3")
        o4 = lists.tile([P, M // 16], U16, name="o4")

        banks = [psum.tile([P, BANK], F32, name="bank%d" % n) for n in range(8)]

        def held(name, width, dtype):
            return keep.tile([P, width], dtype, name=name, align_bytes=64)

        def placed(name, width, dtype, kib):
            return shared.tile([P, width], dtype, name=name, align_bytes=64, offset=kib * KB)

        wg = [held("wg%d" % c, S, F32) for c in range(SLICES - 1)] + [placed("wgs", S, F32, 72)]
        h = [held("h%d" % c, S, F32) for c in range(SLICES)]
        vec_rows = held("vec_rows", P, F32)
        ident = held("ident", P, F32)
        cols = held("cols", 4 * SLICES, F32)
        tab_sc = held("tab_sc", T, U8)
        got_sc = held("got_sc", S, U8)
        got = [held("got%d" % a, S, U32) for a in range(PASSES1)]
        w1_codes = [held("w1c%d" % c, PASSES1 * P, U32) for c in range(SLICES)]
        w1_sc = [held("w1s%d" % c, PASSES1 * P, U8) for c in range(SLICES)]
        w2_codes = held("w2c", PASSES2 * 2 * H, U8)
        w2_sc = held("w2s", PASSES2 * H, U8)
        w3_codes = [held("w3c%d" % b, H, U32) for b in range(PASSES2)]
        x_codes = [held("xc%d" % b, M, U32) for b in range(PASSES2)]
        t_codes = [held("tc%d" % b, M, U32) for b in range(PASSES2)]
        work0 = held("work0", 3 * KB, F32)
        work1 = held("work1", 4 * KB, F32)
        stage = held("stage", 3 * KB, F32)

        gain_col, sc_col, tg_col, gf_col = [
            [cols[:, SLICES * v + c: SLICES * v + c + 1] for c in range(SLICES)] for v in range(4)]

        def load_w1(pair, raw):
            for a in range(PASSES1):
                nc.sync.dma_start(
                    out=raw[:, KB * a: KB * (a + 1)].rearrange("p (i n) -> p i n", i=PACK),
                    in_=w1[KP * a: KP * (a + 1), 2 * P * pair: 2 * P * (pair + 1)].rearrange("(p i) n -> p i n", i=PACK))

        def load_page(c, kib):
            page = placed("page%d" % c, T2, F32, kib)
            nc.sync.dma_start(out=page[:], in_=page0[P * c: P * (c + 1), :])
            return page

        def load_table(a, words):
            nc.sync.dma_start(out=words[:].bitcast(I32), in_=tab_words[a].rearrange("p t i -> p (t i)").bitcast(I32))

        def load_vector(v, vec):
            nc.sync.dma_start(out=vec_rows[SLICES * v: SLICES * (v + 1), :], in_=vec.rearrange("(c p) -> c p", p=P))

        def load_w3(b, raw):
            nc.sync.dma_start(out=raw[:], in_=w3[KP * b: KP * (b + 1), :].rearrange("(p i) n -> p (i n)", i=PACK))

        def w1_bf(c):
            width = PASSES1 * KP
            return stage[:].bitcast(BF16)[:, width * (c % 4): width * (c % 4 + 1)]

        def round_w1(pair, raw):
            for s in range(2):
                rows = raw[:, 0: 3 * KB].rearrange("p (a i s c j) -> p s a c i j", a=PASSES1, i=PACK, s=2, j=4)
                nc.scalar.copy(out=w1_bf(2 * pair + s).rearrange("p (a c j i) -> p a c i j", a=PASSES1, j=4, i=PACK),
                               in_=rows[:, s])
            for s in range(2):
                c = 2 * pair + s
                nc.vector.quantize_mx(out=w1_codes[c][:].bitcast(FP8X4), scales=w1_sc[c][:], in_=w1_bf(c))

        def interleave(dst, rows):
            nc.scalar.copy(out=dst.rearrange("p (c j i) -> p c i j", j=4, i=PACK),
                           in_=rows.rearrange("p i (c j) -> p c i j", j=4))

        nc.vector.memset(tab_sc[:].bitcast(I32), 0)
        nc.vector.memset(vec_rows[:], 0.0)
        nc.vector.memset(w2_sc[:].bitcast(I32), 0)
        nc.sync.dma_start(o1[:], offs)
        nc.sync.dma_start(o2[:], offs2)
        nc.sync.dma_start(o3[:], offs3)
        nc.sync.dma_start(o4[:], offs4)
        nc.sync.dma_start(out=wg[SLICES - 1][:], in_=wgs)
        load_w1(0, work0)
        tab = [placed("tab%d" % a, T, U32, 16 * a) for a in range(PASSES1)]
        load_table(0, tab[0])
        load_vector(0, gain)
        for q in range(4):
            nc.sync.dma_start(out=tab_sc[32 * q: 32 * q + 4 * PASSES1, :].bitcast(I32),
                              in_=tab_scales[:, 4 * q: 4 * q + 4, :].bitcast(I32))
        load_table(1, tab[1])
        load_table(2, tab[2])
        pages = {0: load_page(0, 48)}
        load_w1(1, work1)
        pages[1] = load_page(1, 56)

        make_identity(nc, ident[:])
        nc.tensor.transpose(banks[7][:, 0:P], vec_rows[:], ident[:])
        nc.scalar.copy(out=cols[:, 0:SLICES], in_=banks[7][:, 0:SLICES])
        round_w1(0, work0)
        for c in range(SLICES):
            nc.scalar.activation(out=wg[c][:], in_=wg[SLICES - 1][:], func=ACT.Copy, scale=gain_col[c])

        first_pieces = ((0, 256), (256, 512), (512, 1024))
        nc.vector.tensor_copy(out=got_sc[:], in_=tab_sc[:].indirect(o1[:]))
        for a in range(PASSES1 - 1):
            nc.vector.tensor_copy(out=got[a][:], in_=tab[a][:].indirect(o1[:]))
        for lo, hi in first_pieces:
            nc.vector.tensor_copy(out=got[PASSES1 - 1][:, lo:hi],
                                  in_=tab[PASSES1 - 1][:].indirect(o1[:, lo // 16: hi // 16]))

        work2 = placed("work2", 4 * KB, F32, 0)
        load_w1(2, work2)
        pages[2] = load_page(2, 16)
        work3 = placed("work3", 3 * KB, F32, 32)
        load_w1(3, work3)
        pages[3] = load_page(3, 24)
        nc.sync.dma_start(out=w2_codes[:].bitcast(I32).rearrange("p (b n) -> p b n", b=PASSES2),
                          in_=w2_words.rearrange("b p n -> p b n").bitcast(I32))
        for q in range(4):
            nc.sync.dma_start(out=w2_sc[32 * q: 32 * q + 4, :].bitcast(I32).rearrange("r (b n) -> r b n", b=PASSES2),
                              in_=w2_scales[:, 4 * q: 4 * q + 4, :].rearrange("b r n -> r b n").bitcast(I32))
        raws = {1: work1, 2: work2, 3: work3}

        forest = {}
        next_bank = 0
        for c in range(SLICES):
            if c in raws:
                round_w1(c, raws[c])
                mag = raws[c][:, 0:S]
            elif c > 3:
                mag = work3[:, S * (c % 3): S * (c % 3 + 1)]
            else:
                mag = h[c][:]
            pieces = first_pieces if c == 0 else ((0, BANK), (BANK, S))
            for lo, hi in pieces:
                acc = banks[next_bank % 8][:, 0: hi - lo]
                next_bank = next_bank + 1
                for a in range(PASSES1):
                    nc.tensor.matmul_mx(out=acc, lhsT=w1_codes[c][:, P * a: P * (a + 1)].bitcast(FP8X4),
                                        lhsT_scale=w1_sc[c][:, P * a: P * (a + 1)],
                                        rhs=got[a][:, lo:hi].bitcast(FP8X4), rhs_scale=got_sc[4 * a: P, lo:hi],
                                        start=(a == 0), stop=(a == PASSES1 - 1))
                nc.scalar.activation(out=mag[:, lo:hi], in_=acc, func=ACT.Abs)
                if c == 0:
                    nc.scalar.activation(out=h[c][:, lo:hi], in_=mag[:, lo:hi], func=ACT.Ln, bias=1.0)
                    nc.vector.tensor_tensor(pages[c][:].indirect(o2[:, lo // 16: hi // 16]), h[c][:, lo:hi],
                                            wg[c][:, lo:hi], ALU.mult)
            if c > 0:
                nc.scalar.activation(out=h[c][:], in_=mag, func=ACT.Ln, bias=1.0)
                nc.vector.tensor_tensor(pages[c][:].indirect(o2[:]), h[c][:], wg[c][:], ALU.mult)
            nc.vector.tensor_copy(out=h[c][:, 0:M], in_=pages[c][:].indirect(o3[:]))
            if c < 3:
                forest[c] = wg[c][:, 0:M]
                nc.vector.tensor_copy(out=forest[c], in_=pages[c][:].indirect(o4[:]))
            if c == 0:
                pages[4] = load_page(4, 48)
            if c == 1:
                load_w3(0, work1)
                pages[5] = load_page(5, 56)
            if c == 2:
                load_w3(1, work2)
                pages[6] = load_page(6, 16)
                pages[7] = load_page(7, 64)

        for v, vec in enumerate((sc, tg, gf)):
            load_vector(v + 1, vec)
        nc.tensor.transpose(banks[7][:, 0:P], vec_rows[:], ident[:])
        nc.scalar.copy(out=cols[:, SLICES: 4 * SLICES], in_=banks[7][:, SLICES: 4 * SLICES])
        dealt = (work0, stage)
        w3_sc = [placed("w3s%d" % b, H, U8, 72 + b) for b in range(PASSES2)]
        x_sc = [placed("xs0", M, U8, 74), held("xs1", M, U8)]
        t_sc = [placed("ts0", M, U8, 75), held("ts1", M, U8)]
        w3_raw = (work1, work2)

        def tanh_and_deal(c):
            th = work3[:, S: S + M] if c < 4 else work0[:, M: 2 * M]
            nc.scalar.activation(out=th, in_=h[c][:, 0:M], func=ACT.Tanh, scale=sc_col[c])
            nc.scalar.activation(out=h[c][:, M:ROW].bitcast(BF16), in_=th, func=ACT.Copy, scale=tg_col[c])
            q = c % 4
            nc.sync.dma_start(out=dealt[c // 4][32 * q: 32 * (q + 1), :].rearrange("p (i m) -> p i m", i=PACK),
                              in_=h[c][:, 0:ROW])

        def second_stage(b):
            x_bf = work2[:, KB * b: KB * (b + 1)].bitcast(BF16)
            t_bf = work1[:, KB * b: KB * (b + 1)].bitcast(BF16)
            interleave(x_bf, dealt[b][:].rearrange("p (i m) -> p i m", i=PACK)[:, :, 0:M])
            interleave(t_bf, dealt[b][:].bitcast(BF16).rearrange("p (i m) -> p i m", i=PACK)[:, :, 2 * M: 3 * M])
            nc.vector.quantize_mx(out=x_codes[b][:].bitcast(FP8X4), scales=x_sc[b][:], in_=x_bf)
            nc.vector.quantize_mx(out=t_codes[b][:].bitcast(FP8X4), scales=t_sc[b][:], in_=t_bf)
            for n in range(SLICES):
                nc.tensor.matmul_mx(out=banks[n][:],
                                    lhsT=w2_codes[:, 2 * (H * b + P * n): 2 * (H * b + P * (n + 1))].bitcast(FP4X4),
                                    lhsT_scale=w2_sc[:, H * b + P * n: H * b + P * (n + 1)],
                                    rhs=x_codes[b][:].bitcast(FP8X4), rhs_scale=x_sc[b][:],
                                    start=(b == 0), stop=False)
            for n in range(SLICES):
                nc.tensor.matmul_mx(out=banks[n][:], lhsT=w3_codes[b][:, P * n: P * (n + 1)].bitcast(FP8X4),
                                    lhsT_scale=w3_sc[b][:, P * n: P * (n + 1)],
                                    rhs=t_codes[b][:].bitcast(FP8X4), rhs_scale=t_sc[b][:],
                                    start=False, stop=(b == PASSES2 - 1))

        def pick_forest(c, dst):
            forest[c] = dst
            nc.vector.tensor_copy(out=dst, in_=pages[c][:].indirect(o4[:]))

        for c in range(4):
            tanh_and_deal(c)
        w3_bf = [placed("w3bf%d" % b, PACK * H, BF16, 32 + 8 * b) for b in range(PASSES2)]
        for b in range(PASSES2):
            interleave(w3_bf[b][:], w3_raw[b][:].rearrange("p (i n) -> p i n", i=PACK))
            nc.vector.quantize_mx(out=w3_codes[b][:].bitcast(FP8X4), scales=w3_sc[b][:], in_=w3_bf[b][:])
        second_stage(0)
        for c in range(4, SLICES):
            tanh_and_deal(c)
        pick_forest(3, work2[:, 0:M])
        pick_forest(4, work2[:, M: 2 * M])
        pick_forest(5, work1[:, 0:M])
        pick_forest(6, work1[:, M: 2 * M])
        second_stage(1)
        pick_forest(7, work1[:, 2 * M: 3 * M])

        for n in range(SLICES):
            mag = wg[n][:, M:S] if n < SLICES - 1 else wg[n - 1][:, 0:M]
            nc.scalar.activation(out=mag, in_=banks[n][:], func=ACT.Abs)
            nc.vector.scalar_tensor_tensor(out=h[n][:, 0:M], in0=forest[n], scalar=gf_col[n], in1=mag,
                                           op0=ALU.mult, op1=ALU.add)
            nc.sync.dma_start(out=out[P * n: P * (n + 1), :], in_=h[n][:, 0:M])
